import numpy as np
import ml_dtypes


def mxq(x, axis, fmt="e4m3"):
    dtype, down = {"e4m3": (ml_dtypes.float8_e4m3fn, 7), "e5m2": (ml_dtypes.float8_e5m2, 14)}[fmt]
    v = np.moveaxis(np.asarray(x, np.float32).astype(ml_dtypes.bfloat16).astype(np.float64), axis, -1)
    blocks = v.reshape(v.shape[:-1] + (-1, 32))
    amax = np.abs(blocks).max(-1, keepdims=True)
    byte = np.maximum(np.where(amax > 0, np.frexp(amax)[1] - 1 + 127, 0) - down, 1)
    scale = np.exp2(byte - 127.0)
    codes = (blocks / scale).astype(np.float32).astype(dtype).astype(np.float64)
    return np.moveaxis((codes * scale).reshape(v.shape), -1, axis)


WIDE = False


def mx_kscale(k):
    if not WIDE:
        return np.ones(k)
    levels = np.array([10, -10, 5, -5, 0])
    if k % 512:
        return np.exp2(np.random.permutation(np.resize(levels, k // 32))).repeat(32)
    a = np.empty((k // 512, 16))
    for p in range(k // 512):
        a[p, :8] = np.random.permutation(np.resize(levels, 8))
        for g in range(8):
            far = levels[np.abs(levels - a[p, g]) >= 10]
            a[p, g + 8] = far[np.random.randint(len(far))]
    return np.exp2(a.ravel()).repeat(32)


def f64(x):
    return np.asarray(x).astype(np.float64)


def striped8(idx):
    return np.concatenate([v.reshape(-1, 16).T for v in idx]).astype(np.uint16)


def unstriped8(offs):
    return np.stack([offs[16 * g:16 * g + 16].T.reshape(-1) for g in range(8)]).astype(np.int64)


E2M1 = np.array([0.0, 0.5, 1.0, 1.5, 2.0, 3.0, 4.0, 6.0, -0.0, -0.5, -1.0, -1.5, -2.0, -3.0, -4.0, -6.0])


def pack_weight(w, fmt):
    k, n = w.shape
    w = f64(np.asarray(w, np.float32).astype(ml_dtypes.bfloat16)).reshape(k // 32, 32, n)
    amax = np.abs(w).max(1)
    if fmt == "e4m3":
        byte = np.frexp(amax)[1] - 1 + 127 - 7
    else:
        mant, ex = np.frexp(amax / 6.0)
        byte = np.where(mant > 0.5, ex, ex - 1) + 127
    byte = np.clip(np.where(amax > 0, byte, 1), 1, 254)
    scaled = (w * np.exp2(127.0 - byte)[:, None, :]).reshape(k, n).astype(np.float32)
    by_word = np.ascontiguousarray(scaled.reshape(k // 512, 128, 4, n).transpose(0, 1, 3, 2))
    if fmt == "e4m3":
        words = by_word.astype(ml_dtypes.float8_e4m3fn).view(np.uint8)
    else:
        c = by_word.astype(ml_dtypes.float4_e2m1fn).view(np.uint8) & 0xF
        words = (c[..., 0::2] | (c[..., 1::2] << 4)).reshape(k // 512, 128, 2 * n)
    return np.ascontiguousarray(words), np.ascontiguousarray(byte.astype(np.uint8).reshape(k // 512, 16, n))


def unpack_weight(words, scales, fmt):
    g, _, n = scales.shape
    words = np.ascontiguousarray(words).reshape(g, 128, n, -1)
    if fmt == "e4m3":
        vals = words.view(ml_dtypes.float8_e4m3fn).astype(np.float64)
    else:
        nib = np.empty((g, 128, n, 4), np.uint8)
        nib[..., 0::2] = words & 0xF
        nib[..., 1::2] = words >> 4
        vals = E2M1[nib]
    vals = vals * np.repeat(np.exp2(scales.astype(np.float64) - 127.0), 8, axis=1)[..., None]
    return vals.transpose(0, 1, 3, 2).reshape(g * 512, n)


K, M, T, S = 1024, 256, 1024, 512


def setup_inputs():
    n = np.random.standard_normal
    s = mx_kscale(K)[:, None]
    w = n((K, M)) / np.sqrt(K) / s
    w4 = pack_weight(w, "e2m1")
    rest = w - unpack_weight(*w4, "e2m1")
    p_r8 = pack_weight(rest, "e4m3")
    return {
        "xT": (n((K, T)) * s).astype(np.float32),
        "w4_words": w4[0],
        "w4_scales": w4[1],
        "r8_words": p_r8[0],
        "r8_scales": p_r8[1],
        "wgt": np.repeat(np.random.uniform(0.5, 2.0, (8, S)), 16, axis=0).astype(np.float32),
        "r": (n((256, 512))).astype(np.float32),
        "offs": striped8(np.stack([np.random.permutation(T)[:S] for _ in range(8)])),
    }


def reference(xT, w4_words, w4_scales, r8_words, r8_scales, wgt, r, offs):
    idx = unstriped8(offs)
    group = np.arange(K) % 512 // 64
    xg = f64(wgt)[np.arange(K) // 4 % 128] * f64(xT)[np.arange(K)[:, None], idx[group]]
    xT_ = mxq(xg, 0, "e4m3")
    w4_ = unpack_weight(w4_words, w4_scales, "e2m1")
    r8_ = unpack_weight(r8_words, r8_scales, "e4m3")
    y = w4_.T @ xT_ + r8_.T @ xT_
    return f64(r) + y

@@ -1,0 +1,159 @@
+from contextlib import ExitStack
+
+import concourse.mybir as mybir
+
+K, M, T, S = 1024, 256, 1024, 512
+FLOPS = 2 * 2 * K * M * S
+
+F32 = mybir.dt.float32
+BF16 = mybir.dt.bfloat16
+I32 = mybir.dt.int32
+U32 = mybir.dt.uint32
+U16 = mybir.dt.uint16
+U8 = mybir.dt.uint8
+E4M3X4 = mybir.dt.float8_e4m3fn_x4
+E2M1X4 = mybir.dt.float4_e2m1fn_x4
+MULT = mybir.AluOpType.mult
+ADD = mybir.AluOpType.add
+
+P = 128
+PASSES = K // 512
+GROUP = 128
+
+
+def tile_list_heads_res_kernel(tc, xT, w4_words, w4_scales, r8_words, r8_scales, wgt, r, offs, out):
+    nc = tc.nc
+    with ExitStack() as ctx:
+        keep = ctx.enter_context(tc.tile_pool(name="keep", bufs=1))
+        psum = ctx.enter_context(tc.psum_pool(name="psum", bufs=1))
+
+        lists = keep.tile([P, S // 16], U16, name="lists")
+        w4_sc = keep.tile([P, PASSES, M], U8, name="w4_sc", align_bytes=64)
+        r8_sc = keep.tile([P, PASSES, M], U8, name="r8_sc", align_bytes=64)
+        w4_cd = keep.tile([P, PASSES, 2 * M], U8, name="w4_cd", align_bytes=64)
+        r8_cd = keep.tile([P, PASSES, 4 * M], U8, name="r8_cd", align_bytes=64)
+        res = keep.tile([P, M // P, S], F32, name="res")
+        wg = [keep.tile([P, S // 2], F32, name=f"wg{h}") for h in range(2)]
+        x = [[keep.tile([P, T], F32, name=f"x{a}_{i}") for i in range(4)] for a in range(PASSES)]
+        warm = keep.tile([P, 2], F32, name="warm")
+        warm_out = keep.tile([P, 2], BF16, name="warm_out")
+
+        xv = xT.rearrange("(a p i) t -> a p i t", p=P, i=4)
+        nc.sync.dma_start(lists[:], offs)
+        nc.scalar.dma_start(wg[0][:], wgt[:, 0 : S // 2])
+        nc.sync.dma_start(x[0][0][:], xv[0, :, 0, :])
+        nc.sync.dma_start(wg[1][:], wgt[:, S // 2 : S])
+        for a, i in ((0, 1), (0, 2), (0, 3), (1, 0), (1, 1)):
+            nc.sync.dma_start(x[a][i][:], xv[a, :, i, :])
+        nc.sync.dma_start(w4_cd[:].bitcast(I32), w4_words.bitcast(I32).rearrange("a p w -> p a w"))
+        nc.sync.dma_start(r8_cd[:].bitcast(I32), r8_words.rearrange("a p n i -> a p (n i)").bitcast(I32).rearrange("a p w -> p a w"))
+        for a, i in ((1, 2), (1, 3)):
+            nc.sync.dma_start(x[a][i][:], xv[a, :, i, :])
+        nc.sync.dma_start(res[:], r.rearrange("(m p) j -> p m j", p=P))
+
+        nc.vector.memset(w4_sc[:].bitcast(I32), 0)
+        nc.vector.memset(r8_sc[:].bitcast(I32), 0)
+        nc.vector.memset(warm[:], 0.0)
+        nc.scalar.copy(warm_out[:], warm[:])
+        for tile, src in ((w4_sc, w4_scales), (r8_sc, r8_scales)):
+            rows = src.bitcast(I32).rearrange("a q w -> q a w")
+            for q in range(4):
+                nc.gpsimd.dma_start(tile[32 * q : 32 * q + 4, :, :].bitcast(I32), rows[4 * q : 4 * q + 4])
+
+        chunks = {0: (256, 256), 1: (256, 128, 128)}
+        start = {a: [sum(chunks[a][:c]) for c in range(len(chunks[a]))] for a in chunks}
+        gat, grp, cod, sca = {}, {}, {}, {}
+        for a in chunks:
+            for c, n in enumerate(chunks[a]):
+                gat[a, c] = keep.tile([P, 4, n], F32, name=f"gat{a}_{c}")
+                grp[a, c] = keep.tile([P, n, 4], BF16, name=f"grp{a}_{c}", align_bytes=64)
+                cod[a, c] = keep.tile([P, n], U32, name=f"cod{a}_{c}", align_bytes=64)
+                sca[a, c] = keep.tile([P, n], U8, name=f"sca{a}_{c}", align_bytes=64)
+        acc = [[psum.tile([P, GROUP], F32, name=f"acc{m}_{b}") for b in range(S // GROUP)] for m in range(M // P)]
+        res_out = [keep.tile([P, M // P, n], F32, name=f"res_out{c}") for c, n in enumerate(chunks[1])]
+
+        def gather(a, i, c):
+            j0, n = start[a][c], chunks[a][c]
+            h, w0 = j0 // (S // 2), j0 % (S // 2)
+            nc.vector.tensor_tensor(
+                gat[a, c][:, i, :],
+                x[a][i][:].indirect(lists[:, j0 // 16 : (j0 + n) // 16]),
+                wg[h][:, w0 : w0 + n],
+                MULT,
+            )
+
+        def interleave(a, c):
+            nc.scalar.copy(
+                grp[a, c][:].rearrange("p (c i) t -> p c t i", i=4),
+                gat[a, c][:].rearrange("p t (c i) -> p c t i", i=4),
+            )
+
+        def quantise(a, c):
+            nc.vector.quantize_mx(
+                out=cod[a, c][:].bitcast(E4M3X4),
+                scales=sca[a, c][:],
+                in_=grp[a, c][:].rearrange("p n t -> p (n t)"),
+            )
+
+        def multiply(a, c):
+            j0, n = start[a][c], chunks[a][c]
+            for b in range(j0 // GROUP, (j0 + n) // GROUP):
+                cols = slice(b * GROUP - j0, (b + 1) * GROUP - j0)
+                for m in range(M // P):
+                    rhs = cod[a, c][:, cols].bitcast(E4M3X4)
+                    rhs_scale = sca[a, c][:, cols]
+                    nc.tensor.matmul_mx(
+                        out=acc[m][b][:],
+                        lhsT=w4_cd[:, a, 2 * P * m : 2 * P * (m + 1)].bitcast(E2M1X4),
+                        lhsT_scale=w4_sc[:, a, P * m : P * (m + 1)],
+                        rhs=rhs, rhs_scale=rhs_scale, start=(a == 0), stop=False,
+                    )
+                    nc.tensor.matmul_mx(
+                        out=acc[m][b][:],
+                        lhsT=r8_cd[:, a, 4 * P * m : 4 * P * (m + 1)].bitcast(E4M3X4),
+                        lhsT_scale=r8_sc[:, a, P * m : P * (m + 1)],
+                        rhs=rhs, rhs_scale=rhs_scale, start=False, stop=(a == PASSES - 1),
+                    )
+
+        def finish(c, m):
+            j0, n = start[1][c], chunks[1][c]
+            for b in range(j0 // GROUP, (j0 + n) // GROUP):
+                cols = slice(b * GROUP - j0, (b + 1) * GROUP - j0)
+                nc.vector.tensor_tensor(
+                    res_out[c][:, m, cols], acc[m][b][:], res[:, m, b * GROUP : (b + 1) * GROUP], ADD
+                )
+            nc.sync.dma_start(out[P * m : P * (m + 1), j0 : j0 + n], res_out[c][:, m, :])
+
+        for i in range(4):
+            for c in range(2):
+                gather(0, i, c)
+        interleave(0, 0)
+        interleave(0, 1)
+        gather(1, 0, 0)
+        gather(1, 1, 0)
+        quantise(0, 0)
+        multiply(0, 0)
+        gather(1, 2, 0)
+        gather(1, 3, 0)
+        interleave(1, 0)
+        quantise(0, 1)
+        multiply(0, 1)
+        for i in range(4):
+            gather(1, i, 1)
+        interleave(1, 1)
+        gather(1, 0, 2)
+        quantise(1, 0)
+        multiply(1, 0)
+        gather(1, 1, 2)
+        gather(1, 2, 2)
+        quantise(1, 1)
+        multiply(1, 1)
+        gather(1, 3, 2)
+        interleave(1, 2)
+        finish(0, 0)
+        quantise(1, 2)
+        multiply(1, 2)
+        finish(0, 1)
+        for c in (1, 2):
+            for m in range(M // P):
+                finish(c, m)

@@ -43,11 +43,11 @@ def tile_list_heads_res_kernel(tc, xT, w4_words, w4_scales, r8_words, r8_scales,
         nc.scalar.dma_start(wg[0][:], wgt[:, 0 : S // 2])
         nc.sync.dma_start(x[0][0][:], xv[0, :, 0, :])
         nc.sync.dma_start(wg[1][:], wgt[:, S // 2 : S])
-        for a, i in ((0, 1), (0, 2), (0, 3), (1, 0), (1, 1)):
+        for a, i in ((0, 1), (0, 2), (0, 3)):
             nc.sync.dma_start(x[a][i][:], xv[a, :, i, :])
         nc.sync.dma_start(w4_cd[:].bitcast(I32), w4_words.bitcast(I32).rearrange("a p w -> p a w"))
         nc.sync.dma_start(r8_cd[:].bitcast(I32), r8_words.rearrange("a p n i -> a p (n i)").bitcast(I32).rearrange("a p w -> p a w"))
-        for a, i in ((1, 2), (1, 3)):
+        for a, i in ((1, 0), (1, 1), (1, 2), (1, 3)):
             nc.sync.dma_start(x[a][i][:], xv[a, :, i, :])
         nc.sync.dma_start(res[:], r.rearrange("(m p) j -> p m j", p=P))
 
@@ -58,7 +58,7 @@ def tile_list_heads_res_kernel(tc, xT, w4_words, w4_scales, r8_words, r8_scales,
         for tile, src in ((w4_sc, w4_scales), (r8_sc, r8_scales)):
             rows = src.bitcast(I32).rearrange("a q w -> q a w")
             for q in range(4):
-                nc.gpsimd.dma_start(tile[32 * q : 32 * q + 4, :, :].bitcast(I32), rows[4 * q : 4 * q + 4])
+                nc.scalar.dma_start(tile[32 * q : 32 * q + 4, :, :].bitcast(I32), rows[4 * q : 4 * q + 4])
 
         chunks = {0: (256, 256), 1: (256, 128, 128)}
         start = {a: [sum(chunks[a][:c]) for c in range(len(chunks[a]))] for a in chunks}
@@ -87,6 +87,9 @@ def tile_list_heads_res_kernel(tc, xT, w4_words, w4_scales, r8_words, r8_scales,
                 grp[a, c][:].rearrange("p (c i) t -> p c t i", i=4),
                 gat[a, c][:].rearrange("p t (c i) -> p c t i", i=4),
             )
+
+        def interleave_pair(engine_copy, a, c, t):
+            engine_copy(grp[a, c][:, :, t : t + 2], gat[a, c][:, t : t + 2, :].rearrange("p t c -> p c t"))
 
         def quantise(a, c):
             nc.vector.quantize_mx(
@@ -129,31 +132,25 @@ def tile_list_heads_res_kernel(tc, xT, w4_words, w4_scales, r8_words, r8_scales,
                 gather(0, i, c)
         interleave(0, 0)
         interleave(0, 1)
-        gather(1, 0, 0)
-        gather(1, 1, 0)
         quantise(0, 0)
         multiply(0, 0)
-        gather(1, 2, 0)
-        gather(1, 3, 0)
-        interleave(1, 0)
+        for c in range(3):
+            gather(1, 0, c)
         quantise(0, 1)
         multiply(0, 1)
-        for i in range(4):
-            gather(1, i, 1)
-        interleave(1, 1)
-        gather(1, 0, 2)
-        quantise(1, 0)
-        multiply(1, 0)
-        gather(1, 1, 2)
-        gather(1, 2, 2)
-        quantise(1, 1)
-        multiply(1, 1)
-        gather(1, 3, 2)
-        interleave(1, 2)
-        finish(0, 0)
-        quantise(1, 2)
-        multiply(1, 2)
-        finish(0, 1)
-        for c in (1, 2):
+        for c in range(3):
+            gather(1, 1, c)
+        for c in range(3):
+            interleave_pair(nc.scalar.copy, 1, c, 0)
+        for i in (2, 3):
+            for c in range(3):
+                gather(1, i, c)
+        interleave_pair(nc.scalar.copy, 1, 0, 2)
+        interleave_pair(nc.vector.tensor_copy, 1, 1, 2)
+        interleave_pair(nc.scalar.copy, 1, 2, 2)
+        for c in range(3):
+            quantise(1, c)
+            multiply(1, c)
+        for c in range(3):
             for m in range(M // P):
                 finish(c, m)

@@ -28,129 +28,129 @@ def tile_list_heads_res_kernel(tc, xT, w4_words, w4_scales, r8_words, r8_scales,
         psum = ctx.enter_context(tc.psum_pool(name="psum", bufs=1))
 
         lists = keep.tile([P, S // 16], U16, name="lists")
+        wg = keep.tile([P, S], F32, name="wg")
         w4_sc = keep.tile([P, PASSES, M], U8, name="w4_sc", align_bytes=64)
         r8_sc = keep.tile([P, PASSES, M], U8, name="r8_sc", align_bytes=64)
         w4_cd = keep.tile([P, PASSES, 2 * M], U8, name="w4_cd", align_bytes=64)
         r8_cd = keep.tile([P, PASSES, 4 * M], U8, name="r8_cd", align_bytes=64)
         res = keep.tile([P, M // P, S], F32, name="res")
-        wg = [keep.tile([P, S // 2], F32, name=f"wg{h}") for h in range(2)]
         x = [[keep.tile([P, T], F32, name=f"x{a}_{i}") for i in range(4)] for a in range(PASSES)]
         warm = keep.tile([P, 2], F32, name="warm")
         warm_out = keep.tile([P, 2], BF16, name="warm_out")
+        gat = [keep.tile([P, 4, S], F32, name=f"gat{a}") for a in range(PASSES)]
+        grp = [keep.tile([P, S, 4], BF16, name=f"grp{a}", align_bytes=64) for a in range(PASSES)]
+        cod = [keep.tile([P, S], U32, name=f"cod{a}", align_bytes=64) for a in range(PASSES)]
+        sca = [keep.tile([P, S], U8, name=f"sca{a}", align_bytes=64) for a in range(PASSES)]
+        acc = [[psum.tile([P, GROUP], F32, name=f"acc{m}_{b}") for b in range(S // GROUP)] for m in range(M // P)]
+        res_out = [[keep.tile([P, GROUP], F32, name=f"res_out{m}_{b}") for b in range(S // GROUP)] for m in range(M // P)]
 
         xv = xT.rearrange("(a p i) t -> a p i t", p=P, i=4)
-        nc.sync.dma_start(lists[:], offs)
-        nc.scalar.dma_start(wg[0][:], wgt[:, 0 : S // 2])
-        nc.sync.dma_start(x[0][0][:], xv[0, :, 0, :])
-        nc.sync.dma_start(wg[1][:], wgt[:, S // 2 : S])
-        for a, i in ((0, 1), (0, 2), (0, 3)):
+
+        def load_x(a, i):
             nc.sync.dma_start(x[a][i][:], xv[a, :, i, :])
-        nc.sync.dma_start(w4_cd[:].bitcast(I32), w4_words.bitcast(I32).rearrange("a p w -> p a w"))
-        nc.sync.dma_start(r8_cd[:].bitcast(I32), r8_words.rearrange("a p n i -> a p (n i)").bitcast(I32).rearrange("a p w -> p a w"))
-        for a, i in ((1, 0), (1, 1), (1, 2), (1, 3)):
-            nc.sync.dma_start(x[a][i][:], xv[a, :, i, :])
-        nc.sync.dma_start(res[:], r.rearrange("(m p) j -> p m j", p=P))
+
+        def load_scales(tile, src):
+            rows = src.bitcast(I32).rearrange("a q w -> q a w")
+            for q in range(4):
+                nc.sync.dma_start(tile[32 * q : 32 * q + 4, :, :].bitcast(I32), rows[4 * q : 4 * q + 4])
 
         nc.vector.memset(w4_sc[:].bitcast(I32), 0)
         nc.vector.memset(r8_sc[:].bitcast(I32), 0)
         nc.vector.memset(warm[:], 0.0)
+        load_x(0, 0)
+        nc.sync.dma_start(lists[:], offs)
+        nc.scalar.dma_start(wg[:, 384:512], wgt[:, 384:512])
+        nc.sync.dma_start(wg[:, 0:384], wgt[:, 0:384])
+        load_x(0, 1)
+        load_x(0, 2)
+        load_x(0, 3)
+        load_x(1, 0)
+        load_x(1, 1)
+        load_x(1, 2)
+        load_x(1, 3)
+        nc.sync.dma_start(w4_cd[:].bitcast(I32), w4_words.bitcast(I32).rearrange("a p w -> p a w"))
+        nc.sync.dma_start(r8_cd[:].bitcast(I32), r8_words.rearrange("a p n i -> a p (n i)").bitcast(I32).rearrange("a p w -> p a w"))
+        load_scales(w4_sc, w4_scales)
+        load_scales(r8_sc, r8_scales)
+        nc.sync.dma_start(res[:], r.rearrange("(m p) j -> p m j", p=P))
         nc.scalar.copy(warm_out[:], warm[:])
-        for tile, src in ((w4_sc, w4_scales), (r8_sc, r8_scales)):
-            rows = src.bitcast(I32).rearrange("a q w -> q a w")
-            for q in range(4):
-                nc.scalar.dma_start(tile[32 * q : 32 * q + 4, :, :].bitcast(I32), rows[4 * q : 4 * q + 4])
 
-        chunks = {0: (256, 256), 1: (256, 128, 128)}
-        start = {a: [sum(chunks[a][:c]) for c in range(len(chunks[a]))] for a in chunks}
-        gat, grp, cod, sca = {}, {}, {}, {}
-        for a in chunks:
-            for c, n in enumerate(chunks[a]):
-                gat[a, c] = keep.tile([P, 4, n], F32, name=f"gat{a}_{c}")
-                grp[a, c] = keep.tile([P, n, 4], BF16, name=f"grp{a}_{c}", align_bytes=64)
-                cod[a, c] = keep.tile([P, n], U32, name=f"cod{a}_{c}", align_bytes=64)
-                sca[a, c] = keep.tile([P, n], U8, name=f"sca{a}_{c}", align_bytes=64)
-        acc = [[psum.tile([P, GROUP], F32, name=f"acc{m}_{b}") for b in range(S // GROUP)] for m in range(M // P)]
-        res_out = [keep.tile([P, M // P, n], F32, name=f"res_out{c}") for c, n in enumerate(chunks[1])]
-
-        def gather(a, i, c):
-            j0, n = start[a][c], chunks[a][c]
-            h, w0 = j0 // (S // 2), j0 % (S // 2)
+        def gather(a, i, j0, j1):
             nc.vector.tensor_tensor(
-                gat[a, c][:, i, :],
-                x[a][i][:].indirect(lists[:, j0 // 16 : (j0 + n) // 16]),
-                wg[h][:, w0 : w0 + n],
+                gat[a][:, i, j0:j1],
+                x[a][i][:].indirect(lists[:, j0 // 16 : j1 // 16]),
+                wg[:, j0:j1],
                 MULT,
             )
 
-        def interleave(a, c):
-            nc.scalar.copy(
-                grp[a, c][:].rearrange("p (c i) t -> p c t i", i=4),
-                gat[a, c][:].rearrange("p t (c i) -> p c t i", i=4),
-            )
+        def interleave_pair(engine_copy, a, t, j0, j1):
+            engine_copy(grp[a][:, j0:j1, t : t + 2], gat[a][:, t : t + 2, j0:j1].rearrange("p t c -> p c t"))
 
-        def interleave_pair(engine_copy, a, c, t):
-            engine_copy(grp[a, c][:, :, t : t + 2], gat[a, c][:, t : t + 2, :].rearrange("p t c -> p c t"))
-
-        def quantise(a, c):
+        def quantise(a, j0, j1):
             nc.vector.quantize_mx(
-                out=cod[a, c][:].bitcast(E4M3X4),
-                scales=sca[a, c][:],
-                in_=grp[a, c][:].rearrange("p n t -> p (n t)"),
+                out=cod[a][:, j0:j1].bitcast(E4M3X4),
+                scales=sca[a][:, j0:j1],
+                in_=grp[a][:, j0:j1, :].rearrange("p n t -> p (n t)"),
             )
 
-        def multiply(a, c):
-            j0, n = start[a][c], chunks[a][c]
-            for b in range(j0 // GROUP, (j0 + n) // GROUP):
-                cols = slice(b * GROUP - j0, (b + 1) * GROUP - j0)
-                for m in range(M // P):
-                    rhs = cod[a, c][:, cols].bitcast(E4M3X4)
-                    rhs_scale = sca[a, c][:, cols]
-                    nc.tensor.matmul_mx(
-                        out=acc[m][b][:],
-                        lhsT=w4_cd[:, a, 2 * P * m : 2 * P * (m + 1)].bitcast(E2M1X4),
-                        lhsT_scale=w4_sc[:, a, P * m : P * (m + 1)],
-                        rhs=rhs, rhs_scale=rhs_scale, start=(a == 0), stop=False,
-                    )
-                    nc.tensor.matmul_mx(
-                        out=acc[m][b][:],
-                        lhsT=r8_cd[:, a, 4 * P * m : 4 * P * (m + 1)].bitcast(E4M3X4),
-                        lhsT_scale=r8_sc[:, a, P * m : P * (m + 1)],
-                        rhs=rhs, rhs_scale=rhs_scale, start=False, stop=(a == PASSES - 1),
-                    )
+        def multiply_w4(a, m, b):
+            cols = slice(b * GROUP, (b + 1) * GROUP)
+            nc.tensor.matmul_mx(
+                out=acc[m][b][:],
+                lhsT=w4_cd[:, a, 2 * P * m : 2 * P * (m + 1)].bitcast(E2M1X4),
+                lhsT_scale=w4_sc[:, a, P * m : P * (m + 1)],
+                rhs=cod[a][:, cols].bitcast(E4M3X4), rhs_scale=sca[a][:, cols],
+                start=(a == 0), stop=False,
+            )
 
-        def finish(c, m):
-            j0, n = start[1][c], chunks[1][c]
-            for b in range(j0 // GROUP, (j0 + n) // GROUP):
-                cols = slice(b * GROUP - j0, (b + 1) * GROUP - j0)
-                nc.vector.tensor_tensor(
-                    res_out[c][:, m, cols], acc[m][b][:], res[:, m, b * GROUP : (b + 1) * GROUP], ADD
-                )
-            nc.sync.dma_start(out[P * m : P * (m + 1), j0 : j0 + n], res_out[c][:, m, :])
+        def multiply_r8(a, m, b):
+            cols = slice(b * GROUP, (b + 1) * GROUP)
+            nc.tensor.matmul_mx(
+                out=acc[m][b][:],
+                lhsT=r8_cd[:, a, 4 * P * m : 4 * P * (m + 1)].bitcast(E4M3X4),
+                lhsT_scale=r8_sc[:, a, P * m : P * (m + 1)],
+                rhs=cod[a][:, cols].bitcast(E4M3X4), rhs_scale=sca[a][:, cols],
+                start=False, stop=(a == PASSES - 1),
+            )
+
+        def finish(m, b):
+            cols = slice(b * GROUP, (b + 1) * GROUP)
+            nc.vector.tensor_tensor(res_out[m][b][:], acc[m][b][:], res[:, m, cols], ADD)
+            nc.sync.dma_start(out[P * m : P * (m + 1), cols], res_out[m][b][:])
 
         for i in range(4):
-            for c in range(2):
-                gather(0, i, c)
-        interleave(0, 0)
-        interleave(0, 1)
-        quantise(0, 0)
-        multiply(0, 0)
-        for c in range(3):
-            gather(1, 0, c)
-        quantise(0, 1)
-        multiply(0, 1)
-        for c in range(3):
-            gather(1, 1, c)
-        for c in range(3):
-            interleave_pair(nc.scalar.copy, 1, c, 0)
-        for i in (2, 3):
-            for c in range(3):
-                gather(1, i, c)
-        interleave_pair(nc.scalar.copy, 1, 0, 2)
-        interleave_pair(nc.vector.tensor_copy, 1, 1, 2)
-        interleave_pair(nc.scalar.copy, 1, 2, 2)
-        for c in range(3):
-            quantise(1, c)
-            multiply(1, c)
-        for c in range(3):
+            gather(0, i, 384, 512)
+            gather(0, i, 0, 384)
+            if i % 2:
+                interleave_pair(nc.scalar.copy, 0, i - 1, 0, 256)
+                interleave_pair(nc.scalar.copy, 0, i - 1, 256, 512)
+        for i in range(2):
+            for h in range(2):
+                gather(1, i, 256 * h, 256 * (h + 1))
+        interleave_pair(nc.scalar.copy, 1, 0, 0, 512)
+        quantise(0, 0, 256)
+        quantise(0, 256, 512)
+        for m in range(M // P):
+            for b in range(S // GROUP):
+                multiply_w4(0, m, b)
+                multiply_r8(0, m, b)
+        gather(1, 2, 0, 256)
+        gather(1, 3, 0, 256)
+        interleave_pair(nc.scalar.copy, 1, 2, 0, 256)
+        gather(1, 2, 256, 512)
+        quantise(1, 0, 256)
+        for m in range(M // P):
+            for b in (0, 1):
+                multiply_w4(1, m, b)
+                multiply_r8(1, m, b)
+        gather(1, 3, 256, 512)
+        interleave_pair(nc.vector.tensor_copy, 1, 2, 256, 384)
+        interleave_pair(nc.scalar.copy, 1, 2, 384, 512)
+        for b in (2, 3):
+            quantise(1, 128 * b, 128 * (b + 1))
             for m in range(M // P):
-                finish(c, m)
+                multiply_w4(1, m, b)
+                multiply_r8(1, m, b)
+        for b in range(S // GROUP):
+            for m in range(M // P):
+                finish(m, b)

from contextlib import ExitStack

import concourse.mybir as mybir

K, M, T, S = 1024, 256, 1024, 512
FLOPS = 2 * 2 * K * M * S

F32 = mybir.dt.float32
BF16 = mybir.dt.bfloat16
I32 = mybir.dt.int32
U32 = mybir.dt.uint32
U16 = mybir.dt.uint16
U8 = mybir.dt.uint8
E4M3X4 = mybir.dt.float8_e4m3fn_x4
E2M1X4 = mybir.dt.float4_e2m1fn_x4
MULT = mybir.AluOpType.mult
ADD = mybir.AluOpType.add

P = 128
PASSES = K // 512
GROUP = 128


def tile_list_heads_res_kernel(tc, xT, w4_words, w4_scales, r8_words, r8_scales, wgt, r, offs, out):
    nc = tc.nc
    with ExitStack() as ctx:
        keep = ctx.enter_context(tc.tile_pool(name="keep", bufs=1))
        psum = ctx.enter_context(tc.psum_pool(name="psum", bufs=1))

        lists = keep.tile([P, S // 16], U16, name="lists")
        wg = keep.tile([P, S], F32, name="wg")
        w4_sc = keep.tile([P, PASSES, M], U8, name="w4_sc", align_bytes=64)
        r8_sc = keep.tile([P, PASSES, M], U8, name="r8_sc", align_bytes=64)
        w4_cd = keep.tile([P, PASSES, 2 * M], U8, name="w4_cd", align_bytes=64)
        r8_cd = keep.tile([P, PASSES, 4 * M], U8, name="r8_cd", align_bytes=64)
        res = keep.tile([P, M // P, S], F32, name="res")
        x = [[keep.tile([P, T], F32, name=f"x{a}_{i}") for i in range(4)] for a in range(PASSES)]
        warm = keep.tile([P, 2], F32, name="warm")
        warm_out = keep.tile([P, 2], BF16, name="warm_out")
        gat = [keep.tile([P, 4, S], F32, name=f"gat{a}") for a in range(PASSES)]
        grp = [keep.tile([P, S, 4], BF16, name=f"grp{a}", align_bytes=64) for a in range(PASSES)]
        cod = [keep.tile([P, S], U32, name=f"cod{a}", align_bytes=64) for a in range(PASSES)]
        sca = [keep.tile([P, S], U8, name=f"sca{a}", align_bytes=64) for a in range(PASSES)]
        acc = [[psum.tile([P, GROUP], F32, name=f"acc{m}_{b}") for b in range(S // GROUP)] for m in range(M // P)]
        res_out = [[keep.tile([P, GROUP], F32, name=f"res_out{m}_{b}") for b in range(S // GROUP)] for m in range(M // P)]

        xv = xT.rearrange("(a p i) t -> a p i t", p=P, i=4)

        def load_x(a, i):
            nc.sync.dma_start(x[a][i][:], xv[a, :, i, :])

        def load_scales(tile, src):
            rows = src.bitcast(I32).rearrange("a q w -> q a w")
            for q in range(4):
                nc.sync.dma_start(tile[32 * q : 32 * q + 4, :, :].bitcast(I32), rows[4 * q : 4 * q + 4])

        nc.vector.memset(w4_sc[:].bitcast(I32), 0)
        nc.vector.memset(r8_sc[:].bitcast(I32), 0)
        nc.vector.memset(warm[:], 0.0)
        load_x(0, 0)
        nc.sync.dma_start(lists[:], offs)
        nc.scalar.dma_start(wg[:, 384:512], wgt[:, 384:512])
        nc.sync.dma_start(wg[:, 0:384], wgt[:, 0:384])
        load_x(0, 1)
        load_x(0, 2)
        load_x(0, 3)
        load_x(1, 0)
        load_x(1, 1)
        load_x(1, 2)
        load_x(1, 3)
        nc.sync.dma_start(w4_cd[:].bitcast(I32), w4_words.bitcast(I32).rearrange("a p w -> p a w"))
        nc.sync.dma_start(r8_cd[:].bitcast(I32), r8_words.rearrange("a p n i -> a p (n i)").bitcast(I32).rearrange("a p w -> p a w"))
        load_scales(w4_sc, w4_scales)
        load_scales(r8_sc, r8_scales)
        nc.sync.dma_start(res[:], r.rearrange("(m p) j -> p m j", p=P))
        nc.scalar.copy(warm_out[:], warm[:])

        def gather(a, i, j0, j1):
            nc.vector.tensor_tensor(
                gat[a][:, i, j0:j1],
                x[a][i][:].indirect(lists[:, j0 // 16 : j1 // 16]),
                wg[:, j0:j1],
                MULT,
            )

        def interleave_pair(engine_copy, a, t, j0, j1):
            engine_copy(grp[a][:, j0:j1, t : t + 2], gat[a][:, t : t + 2, j0:j1].rearrange("p t c -> p c t"))

        def quantise(a, j0, j1):
            nc.vector.quantize_mx(
                out=cod[a][:, j0:j1].bitcast(E4M3X4),
                scales=sca[a][:, j0:j1],
                in_=grp[a][:, j0:j1, :].rearrange("p n t -> p (n t)"),
            )

        def multiply_w4(a, m, b):
            cols = slice(b * GROUP, (b + 1) * GROUP)
            nc.tensor.matmul_mx(
                out=acc[m][b][:],
                lhsT=w4_cd[:, a, 2 * P * m : 2 * P * (m + 1)].bitcast(E2M1X4),
                lhsT_scale=w4_sc[:, a, P * m : P * (m + 1)],
                rhs=cod[a][:, cols].bitcast(E4M3X4), rhs_scale=sca[a][:, cols],
                start=(a == 0), stop=False,
            )

        def multiply_r8(a, m, b):
            cols = slice(b * GROUP, (b + 1) * GROUP)
            nc.tensor.matmul_mx(
                out=acc[m][b][:],
                lhsT=r8_cd[:, a, 4 * P * m : 4 * P * (m + 1)].bitcast(E4M3X4),
                lhsT_scale=r8_sc[:, a, P * m : P * (m + 1)],
                rhs=cod[a][:, cols].bitcast(E4M3X4), rhs_scale=sca[a][:, cols],
                start=False, stop=(a == PASSES - 1),
            )

        def finish(m, b):
            cols = slice(b * GROUP, (b + 1) * GROUP)
            nc.vector.tensor_tensor(res_out[m][b][:], acc[m][b][:], res[:, m, cols], ADD)
            nc.sync.dma_start(out[P * m : P * (m + 1), cols], res_out[m][b][:])

        for i in range(4):
            gather(0, i, 384, 512)
            gather(0, i, 0, 384)
            if i % 2:
                interleave_pair(nc.scalar.copy, 0, i - 1, 0, 256)
                interleave_pair(nc.scalar.copy, 0, i - 1, 256, 512)
        for i in range(2):
            for h in range(2):
                gather(1, i, 256 * h, 256 * (h + 1))
        interleave_pair(nc.scalar.copy, 1, 0, 0, 512)
        quantise(0, 0, 256)
        quantise(0, 256, 512)
        for m in range(M // P):
            for b in range(S // GROUP):
                multiply_w4(0, m, b)
                multiply_r8(0, m, b)
        gather(1, 2, 0, 256)
        gather(1, 3, 0, 256)
        interleave_pair(nc.scalar.copy, 1, 2, 0, 256)
        gather(1, 2, 256, 512)
        quantise(1, 0, 256)
        for m in range(M // P):
            for b in (0, 1):
                multiply_w4(1, m, b)
                multiply_r8(1, m, b)
        gather(1, 3, 256, 512)
        interleave_pair(nc.vector.tensor_copy, 1, 2, 256, 384)
        interleave_pair(nc.scalar.copy, 1, 2, 384, 512)
        for b in (2, 3):
            quantise(1, 128 * b, 128 * (b + 1))
            for m in range(M // P):
                multiply_w4(1, m, b)
                multiply_r8(1, m, b)
        for b in range(S // GROUP):
            for m in range(M // P):
                finish(m, b)
